import numpy as np, ml_dtypes
CORES = [24,25,26,27,28,29,30,31]
N = 8
BF = ml_dtypes.bfloat16
def gentries(a):
    return np.ascontiguousarray(a.reshape(8, 16, -1).transpose(0, 2, 1)).reshape(8, -1)
def gtable(e):
    e = np.asarray(e); return np.ascontiguousarray(e.reshape(8, -1, 16).transpose(0, 2, 1)).reshape(128, -1).astype(np.int32)
V, G, CAP, D, SH, RO = 2048, 256, 64, 2, 2, 4
def parts(rng):
    t = rng.integers(2 ** 18, 2 ** 19, (N, 8, 16, 1))
    r = np.minimum((t * rng.random((N, 8, 1, V)) * rng.random((N, 8, 16, V))).astype(np.int64), t - 1)
    nb = rng.integers(0, V + (N - 1) * G, (N, 8, D * V)); snd = np.argsort(rng.random((N, 8, N - 1, V)), axis=-1)[..., :G]
    return t, r, nb, np.ascontiguousarray(snd)
def heat(rng, t, r, share):
    m = (rng.random((N, 8, 1, V)) < share) & (rng.random(r.shape) < rng.random((N, 8, 1, V)))
    return np.where(m, np.minimum(t + ((2 ** 20 - t) * rng.random(r.shape)).astype(np.int64), 2 ** 20 - 1), r)
def pack(t, r, nb, snd):
    return {"r0": np.ascontiguousarray(r.reshape(N, 128, V)).astype(np.int32), "th": np.ascontiguousarray(t.reshape(N, 128, 1)).astype(np.int32),
            "nb": np.stack([gtable(a) for a in nb]), "snd": np.stack([gtable(a.reshape(8, -1)) for a in snd])}
def setup_inputs(rng):
    t, r, nb, snd = parts(rng); share = rng.choice(np.array([0.05, 0.15, 0.3, 0.5]), (N, 8, 1, 1))
    return pack(t, heat(rng, t, r, share), nb, snd)
def setup_inputs_room(rng):
    t, r, nb, snd = parts(rng); h = V // 2
    for q in range(N):
        for g in range(8):
            o = rng.permutation(V); a, b = o[:h], o[h:]; i = rng.integers(0, 16, h); lo = t[q, g, i, 0]
            r[q, g, i, a] = np.where(rng.random(h) < 0.5, lo, np.minimum(lo + ((2 ** 20 - lo) * rng.random(h)).astype(np.int64), 2 ** 20 - 1))
            for d in range(N - 1):
                n = int(rng.choice(np.array([0, 1, CAP - 1, CAP, CAP + 1, G])))
                if q == 0 and d == 0: n = (CAP, CAP + 1, G, CAP - 1, 1, 0, CAP, CAP + 1)[g]
                snd[q, g, d] = rng.permutation(np.concatenate([rng.permutation(a)[:n], rng.permutation(b)[:G - n]]))
    return pack(t, r, nb, snd)
def setup_inputs_ties(rng):
    t, r, nb, snd = parts(rng)
    base = rng.choice(np.array([1, 4, 7, 1000, 2 ** 16 - 1, 2 ** 19, 2 ** 20 - 1]), (N, 8, 1, 1)); base[0, 0] = 1; base[0, 1] = 2 ** 19; base[1, 0] = 2 ** 20 - 1
    t = np.minimum(base + rng.integers(0, 3, (N, 8, 16, 1)), 2 ** 20)
    r = (t - 1) * rng.integers(0, 2, (N, 8, 16, V)); hit = rng.random((N, 8, 1, V)) < 0.2
    r = np.where(hit, np.minimum(t - 1 + rng.integers(0, 3, r.shape), 2 ** 20 - 1), r)
    m = rng.permutation(V)[None, :]
    r[0, 0] = np.where(m < 3 * V // 10, t[0, 0], np.where(m < 6 * V // 10, rng.integers(2 ** 19, 2 ** 20, (16, V)), t[0, 0] - 1))
    return pack(t, r, nb, snd)
def setup_inputs_alike(rng):
    t, r, nb, snd = parts(rng); r = heat(rng, t, r, 0.2); r[..., 0] = 2 ** 20 - 1; r[..., V - 1] = 2 ** 20 - 1
    snd[:, ::2] = rng.choice(np.array([0, V - 1, V // 2, 3]), (N, 4, N - 1, G))
    nb[:, 1::2] = np.tile(nb[:, 1::2, :V], (1, 1, D))
    nb[:, 2] = rng.integers(V, V + (N - 1) * G, (N, D * V)); nb[:, 4] = rng.integers(0, V, (N, D * V))
    nb[:, 6] = rng.choice(np.array([0, V - 1, V, V + (N - 1) * G - 1]), (N, D * V))
    return pack(t, r, nb, snd)
def setup_inputs_cold(rng):
    t, r, nb, snd = parts(rng); share = rng.choice(np.array([0.1, 0.25, 0.4]), (N, 8, 1, 1))
    q = rng.permutation(N); share[q[0]] = 1.0; share[q[1]] = 0.0; share[:, rng.integers(0, 8)] = 0.0
    return pack(t, heat(rng, t, r, share), nb, snd)
def setup_inputs_spread(rng):
    t, r, nb, snd = parts(rng)
    t = np.minimum(np.maximum(np.exp2(10 + 10 * rng.random((N, 8, 16, 1))).astype(np.int64), 1), 2 ** 20)
    r = np.minimum((np.exp2(20 * rng.random((N, 8, 1, V))) * rng.random((N, 8, 16, V))).astype(np.int64), 2 ** 20 - 1)
    return pack(t, r, nb, snd)
def check_inputs(d):
    bad = []
    for k, lo, hi in (("r0", 0, 2 ** 20 - 1), ("th", 1, 2 ** 20), ("nb", 0, V + (N - 1) * G - 1), ("snd", 0, V - 1)):
        if np.min(d[k]) < lo or np.max(d[k]) > hi: bad.append("range of " + k)
    return bad
def reference(r0, th, nb, snd):
    r = r0.astype(np.int64).reshape(N, 8, 16, V); t = th.astype(np.int64).reshape(N, 8, 16, 1); p = np.zeros((N, 8, 16, V), np.int64)
    nbl = np.stack([gentries(a) for a in nb]).astype(np.int64); sl = np.stack([gentries(a) for a in snd]).astype(np.int64).reshape(N, 8, N - 1, G)
    for rnd in range(RO):
        over = r >= t; s = np.where(over, r >> SH, 0)
        p = p + np.where(over, r - D * s, 0); r = np.where(over, 0, r)
        hot = np.any(over, axis=2)
        come = []
        for a in range(N):
            w = [s[a]]
            for d in range(1, N):
                q = (a - d) % N; ix = sl[q, :, d - 1]
                h = np.take_along_axis(hot[q], ix, 1).astype(np.int64); before = np.add.accumulate(h, axis=1) - h
                v = np.take_along_axis(s[q], ix[:, None, :], 2)
                w.append(np.where(((h == 1) & (before < CAP))[:, None, :], v, 0))
            w = np.concatenate(w, axis=2)
            come.append(np.add.reduce(np.take_along_axis(w, nbl[a][:, None, :], 2).reshape(8, 16, D, V), axis=2))
        r = r + np.stack(come)
    return {"yp": p.reshape(N, 128, V).astype(np.float32), "yr": r.reshape(N, 128, V).astype(np.float32)}

@@ -1,0 +1,352 @@
+import numpy as np
+from concourse.bass import DstId, RemoteDMATransfer
+from concourse.mybir import AluOpType, ActivationFunctionType
+
+V, G, N, RO = 2048, 256, 8, 4
+NS = (N - 1) * G
+SCRATCH = {
+    "r0i": ("sbuf", [128, V], "int32"),
+    "thi": ("sbuf", [128, 1], "int32"),
+    "thb": ("sbuf", [128, 1], "float32"),
+    "nbi": ("sbuf", [128, 256], "int32"),
+    "nbu": ("sbuf", [128, 256], "uint16"),
+    "sni": ("sbuf", [128, 112], "int32"),
+    "snu": ("sbuf", [128, 112], "uint16"),
+    "one": ("sbuf", [128, 128], "bfloat16"),
+    "blk1": ("sbuf", [128, 128], "bfloat16"),
+    "blk": ("sbuf", [128, 128], "bfloat16"),
+    "base": ("sbuf", [128, 512], "bfloat16"),
+    "RA": ("sbuf", [128, V], "float32"),
+    "RB": ("sbuf", [128, V], "float32"),
+    "X": ("sbuf", [128, V], "float32"),
+    "TT": ("sbuf", [128, V], "float32"),
+    "U0": ("sbuf", [128, V], "float32"),
+    "U1": ("sbuf", [128, V], "float32"),
+    "E0": ("sbuf", [128, V], "float32"),
+    "E1": ("sbuf", [128, V], "float32"),
+    "gs": ("sbuf", [128, NS], "bfloat16"),
+    "hb": ("sbuf", [128, NS], "bfloat16"),
+    "st": ("sbuf", [128, NS], "bfloat16"),
+    "ob0": ("sbuf", [128, NS], "float32"),
+    "ob1": ("sbuf", [128, NS], "float32"),
+    "W0": ("sbuf", [128, V + NS], "float32"),
+    "W1": ("sbuf", [128, V + NS], "float32"),
+    "W2": ("sbuf", [128, V + NS], "float32"),
+    "W3": ("sbuf", [128, V + NS], "float32"),
+    "AB": ("psum", [128, V], "float32"),
+    "hot": ("psum", [128, V], "float32"),
+}
+SEMAPHORES = (["vq", "sq", "pq", "gq", "lsa", "lsb", "lth", "lsn", "lnb", "outp", "outr"] + ["lr%d" % c for c in range(4)]
+              + ["arr%d" % t for t in range(RO)] + ["acc%d" % k for k in range(2 * RO)])
+
+STAGES = ((0, 1), (1, 2), (3, 2), (5, 2))
+
+
+def order(q, T, topo):
+    far = [d for d in range(1, N) if topo.die(T.cores[(q + d) % N]) != topo.die(T.cores[q])]
+    near = [d for d in range(1, N) if d not in far]
+    far.sort(key=lambda d: abs(d - N // 2))
+    o = []
+    for k in range(N):
+        if k < len(far):
+            o.append(far[k])
+        if k < len(near):
+            o.append(near[k])
+    return o
+
+
+def lanes(q, T, topo):
+    o, res = order(q, T, topo), {}
+    for first, n in STAGES:
+        for k in range(n):
+            e = topo.engines(T.cores[q], T.cores[(q + o[first + k]) % N])
+            res[o[first + k]] = e[k::n]
+    return res
+
+
+def rank_program(g, core, T, topo):
+    q = T.rank_of(core)
+    if q is None:
+        return
+    v, s, pe, sy = g.vector, g.scalar, g.tensor, g.sync
+    eng = {"g": g, "v": v, "s": s, "p": pe, "y": sy}
+    cnt, seen = {}, {}
+    op, fn = AluOpType, ActivationFunctionType
+    LAM = 2.0 ** -21
+
+    def need(k, *toks):
+        for name, val in toks:
+            if seen.get((k, name), 0) < val:
+                eng[k].wait_ge(T.sem[name], val)
+                seen[(k, name)] = val
+
+    def fin(ins, name, n=1):
+        cnt[name] = cnt.get(name, 0) + n
+        ins.then_inc(T.sem[name], n)
+        return (name, cnt[name])
+
+    o, lane = order(q, T, topo), lanes(q, T, topo)
+    arrive = sum(len(lanes((q - d) % N, T, topo)[d]) for d in range(1, N))
+    C = [slice(512 * c, 512 * c + 512) for c in range(4)]
+    W = [T["W%d" % t] for t in range(RO)]
+    U, E, OB = [T.U0, T.U1], [T.E0, T.E1], [T.ob0, T.ob1]
+    SC = 2.0 ** 22
+    Q4 = 0.25 * (1.0 - 2.0 ** -23)
+
+    lth = fin(s.dma_start(T.thi[:], T.th[:]), "lth", 16)
+    lr = []
+    for c in range(4):
+        lr.append(fin(sy.dma_start(T.r0i[:, C[c]], T.r0[:, C[c]]), "lr%d" % c, 16))
+    lsn = fin(s.dma_start(T.sni[:], T.snd[:]), "lsn", 16)
+    lnb = fin(s.dma_start(T.nbi[:], T.nb[:]), "lnb", 16)
+    k1 = fin(v.memset(T.one[:], 1.0), "vq")
+    kb = fin(v.memset(T.base[:], 5.0), "vq")
+    need("g", k1)
+    k2 = fin(g.affine_select(T.blk1[:], T.one[:], [[-16, 8], [0, 16]], op.is_ge, 0.0, 0, 1), "gq")
+    need("g", k2)
+    kblk = fin(g.affine_select(T.blk[:], T.blk1[:], [[16, 8], [0, 16]], op.is_ge, 0.0, 15, -1), "gq")
+    need("v", kb)
+    fin(v.memset(T.base[:, 0:1], 69.0), "vq")
+    kbase = fin(v.memset(T.base[:, 256:257], 69.0), "vq")
+    need("v", lth)
+    kth = fin(v.tensor_scalar(T.thb[:], T.thi[:], -2.0, 4.0, op.mult, op.add), "vq")
+    need("v", lsn)
+    ksn = None
+    for k in range(N - 1):
+        d = o[k] - 1
+        ksn = fin(v.tensor_copy(T.snu[:, 16 * k:16 * k + 16], T.sni[:, 16 * d:16 * d + 16]), "vq")
+
+    last = {}
+
+    rt, at, xt, wt = [None] * 4, [None] * 4, [None] * 4, [None] * 4
+
+    def fA(c, R):
+        need("s", kth, rt[c])
+        at[c] = fin(s.activation(T.AB[:, C[c]], R[:, C[c]], fn.Relu, bias=T.thb[:], scale=SC), "sq")
+
+    def fX(c, R):
+        need("v", at[c], rt[c], *last.get(("X", c), ()))
+        xt[c] = fin(v.tensor_tensor(T.X[:, C[c]], R[:, C[c]], T.AB[:, C[c]], op.min), "vq")
+
+    def fW(c, t, vec=False):
+        if vec:
+            need("v", xt[c])
+            wt[c] = fin(v.tensor_scalar(W[t][:, C[c]], T.X[:, C[c]], Q4, 4.0, op.mult, op.add), "vq")
+        else:
+            need("s", xt[c])
+            wt[c] = fin(s.activation(W[t][:, C[c]], T.X[:, C[c]], fn.Identity, bias=4.0, scale=Q4), "sq")
+        last[("X", c)] = (wt[c],)
+
+    gt, pt, et, stt, mt = [None] * 4, [None] * 4, [None] * 4, [None] * 4, [None] * 4
+
+    def cols(i):
+        a, n = STAGES[i]
+        return slice(G * a, G * (a + n)), slice(16 * a, 16 * (a + n)), slice(512 * i, 512 * i + G * n), G * n
+
+    def fGS(i, R):
+        cs, cl, ch, n = cols(i)
+        need("s", ksn, kth, *rt)
+        need("s", *last.get(("gs", i), ()))
+        gt[i] = fin(s.activation(T.gs[:, cs], R[:, 0:V].indirect(T.snu[:, cl]), fn.Relu, bias=T.thb[:], scale=SC), "sq")
+        need("p", kblk, gt[i], *last.get(("hot", i), ()))
+        pt[i] = fin(pe.matmul(T.hot[:, ch], T.blk[:], T.gs[:, cs], True, True), "pq")
+        last[("gs", i)] = (pt[i],)
+
+    def fEV(i, vec):
+        cs, cl, ch, n = cols(i)
+        k = "v" if vec else "s"
+        need(k, pt[i], *last.get(("hb", i), ()))
+        if vec:
+            et[i] = fin(v.tensor_scalar(T.hb[:, cs], T.hot[:, ch], 0.0, None, op.is_gt), "vq")
+        else:
+            et[i] = fin(s.activation(T.hb[:, cs], T.hot[:, ch], fn.Sign), "sq")
+        last[("hot", i)] = (et[i],)
+
+    def fSCAN(i):
+        cs, cl, ch, n = cols(i)
+        need("v", et[i], kbase)
+        stt[i] = fin(v.tensor_tensor_scan(T.st[:, cs], T.base[:, 0:n], T.hb[:, cs], 69.0, op.max, op.subtract), "vq")
+        last[("hb", i)] = (stt[i],)
+
+    def fGM(i, t):
+        cs, cl, ch, n = cols(i)
+        need("v", stt[i], *wt)
+        if t >= 2:
+            need("v", ("ls" + "ab"[t % 2], left[t - 2]))
+        mt[i] = fin(v.tensor_tensor(OB[t % 2][:, cs], W[t][:, 0:V].indirect(T.snu[:, cl]), T.st[:, cs], op.min), "vq")
+
+    left = {}
+
+    def send(i, t):
+        a, n = STAGES[i]
+        need("g", mt[i])
+        ls = "ls" + "ab"[t % 2]
+        tr = []
+        for k in range(n):
+            d = o[a + k]
+            dst = T.cores[(q + d) % N]
+            ad = topo.addr(dst)
+            m = sum(1 << e for e in lane[d])
+            src = OB[t % 2][:, G * (a + k):G * (a + k + 1)]
+            out = W[t][:, V + (d - 1) * G:V + d * G]
+            cnt[ls] = cnt.get(ls, 0) + len(lane[d])
+            if n == 1:
+                g.remote_dma(out, src, T.sem["arr%d" % t], T.sem[ls], ad[1], ad[0], m)
+            else:
+                tr.append(RemoteDMATransfer(dst_ids=[DstId(rid=ad[0], pnc=ad[1])], dma_engine_mask=m,
+                                            remote_sem=T.sem["arr%d" % t], src=src, dst=out))
+        if tr:
+            g.remote_dma_fused(tr, local_sem=T.sem[ls])
+        left[t] = cnt[ls]
+
+    def acc(k, buf, *toks):
+        need("g", *toks)
+        return fin(g.dma_start(T.RA[:], buf[:], accum_op=op.add), "acc%d" % k, 16)
+
+    def slots(t, R, steps):
+        for st in steps:
+            if st[0] == "x":
+                fX(st[1], R)
+            elif st[0] == "w":
+                fW(st[1], t, len(st) > 2)
+            elif st[0] == "a":
+                fA(st[1], R)
+            elif st[0] == "g":
+                fGS(st[1], R)
+            elif st[0] == "e":
+                fEV(st[1], len(st) > 2)
+            elif st[0] == "s":
+                fSCAN(st[1])
+            elif st[0] == "m":
+                fGM(st[1], t)
+                send(st[1], t)
+
+    TAIL = (("w", 3, 1), ("e", 0, 1), ("s", 0), ("m", 0), ("g", 1), ("g", 2), ("e", 1, 1), ("s", 1), ("m", 1),
+            ("e", 2), ("g", 3), ("s", 2), ("m", 2), ("e", 3), ("s", 3), ("m", 3))
+
+    for c in range(4):
+        need("v", lr[c])
+        rt[c] = fin(v.tensor_scalar(T.RA[:, C[c]], T.r0i[:, C[c]], -1.0, LAM, op.add, op.mult), "vq")
+        fA(c, T.RA)
+        fX(c, T.RA)
+        if c < 3:
+            fW(c, 0)
+        else:
+            fGS(0, T.RA)
+    slots(0, T.RA, TAIL)
+    need("v", lnb)
+    knb = fin(v.tensor_copy(T.nbu[:], T.nbi[:]), "vq")
+
+    ae, au = {}, {}
+    for t in range(RO):
+        R = T.RA if t == 0 else T.RB
+        final = t == RO - 1
+        need("v", *at)
+        need("v", *xt)
+        dt_ = fin(v.tensor_tensor(T.AB[:], R[:], T.AB[:], op.subtract), "vq")
+        need("s", *wt)
+        if not final:
+            if t >= 2:
+                need("s", ae[t - 2])
+            e_t = fin(s.activation(E[t % 2][:], W[t][:, 0:V], fn.Identity, bias=16.0 * 1.0 - 8.0, scale=-2.0), "sq")
+        else:
+            need("s", *et)
+            need("s", *pt)
+            e_t = fin(s.activation(T.hot[:], W[t][:, 0:V], fn.Identity, bias=8.0, scale=-2.0), "sq")
+        need("v", dt_)
+        b_t = fin(v.tensor_scalar(T.AB[:], T.AB[:], -LAM, None, op.max), "vq")
+        if not final:
+            ae[t] = acc(2 * t, E[t % 2], e_t, dt_, *([au[t - 1]] if t else []))
+        else:
+            need("v", e_t, au[t - 1], *last[("X", 0)])
+            need("v", *last[("X", 3)])
+            v1 = fin(v.tensor_tensor(T.X[:], T.RA[:], T.hot[:], op.add), "vq")
+            need("v", v1, b_t)
+            v2 = []
+            for c in range(4):
+                v2.append(fin(v.tensor_tensor(T.E0[:, C[c]], T.X[:, C[c]], T.AB[:, C[c]], op.subtract), "vq"))
+        arr = ("arr%d" % t, arrive)
+        ubuf = U[t % 2]
+        utoks = []
+        tt = {}
+
+        def gt1(a, n):
+            need("s", arr, knb, *wt)
+            tt[a] = fin(s.activation(T.TT[:, a:a + n], W[t][:].indirect(T.nbu[:, 128 + a // 16:128 + (a + n) // 16]), fn.Identity,
+                                     bias=-8.0, scale=1.0), "sq")
+
+        def gu(a, n):
+            need("v", arr, knb, *wt)
+            need("v", tt[a])
+            if t >= 2:
+                need("v", au[t - 2])
+            utoks.append(fin(v.tensor_tensor(ubuf[:, a:a + n], W[t][:].indirect(T.nbu[:, a // 16:(a + n) // 16]), T.TT[:, a:a + n],
+                                             op.add), "vq"))
+
+        def fR(c):
+            need("v", b_t, *utoks)
+            rt[c] = fin(v.tensor_tensor(T.RB[:, C[c]], ubuf[:, C[c]], T.AB[:, C[c]], op.add), "vq")
+
+        need("s", *last.get("TT", ()))
+        gt1(0, 256)
+        gt1(256, 256)
+        for c in range(1, 4):
+            gt1(512 * c, 512)
+        gu(0, 256)
+        gu(256, 256)
+        gu(512, 512)
+        fR(0)
+        if not final:
+            RN = T.RB
+            fA(0, RN)
+            gu(1024, 512)
+            fR(1)
+            fA(1, RN)
+            fX(0, RN)
+            fW(0, t + 1)
+            gu(1536, 512)
+            fR(2)
+            fA(2, RN)
+            fX(1, RN)
+            fW(1, t + 1)
+            last["TT"] = (utoks[-1],)
+            fR(3)
+            fA(3, RN)
+            fX(2, RN)
+            fX(3, RN)
+            au[t] = acc(2 * t + 1, ubuf, ae[t], *utoks)
+            fGS(0, RN)
+            fW(2, t + 1)
+            slots(t + 1, RN, TAIL)
+        else:
+            def outp(c):
+                need("s", v2[c])
+                tok = fin(s.activation(T.E1[:, C[c]], T.E0[:, C[c]], fn.Identity, bias=0.0, scale=1.0 / LAM), "sq")
+                need("y", tok)
+                fin(sy.dma_start(T.yp[:, C[c]], T.E1[:, C[c]]), "outp", 16)
+
+            def outr(c):
+                need("s", rt[c])
+                tok = fin(s.activation(T.TT[:, C[c]], T.RB[:, C[c]], fn.Identity, bias=1.0, scale=1.0 / LAM), "sq")
+                need("y", tok)
+                fin(sy.dma_start(T.yr[:, C[c]], T.TT[:, C[c]]), "outr", 16)
+
+            need("s", ae[1], ae[2])
+            outp(0)
+            outr(0)
+            gu(1024, 512)
+            fR(1)
+            outp(1)
+            outr(1)
+            gu(1536, 512)
+            fR(2)
+            outp(2)
+            outr(2)
+            fR(3)
+            outp(3)
+            outr(3)
+    need("y", ("outp", cnt["outp"]), ("outr", cnt["outr"]))
+    for name in ("vq", "sq", "pq", "gq"):
+        need("g", (name, cnt[name]))
+    for name in ("lsa", "lsb"):
+        need("g", (name, cnt[name]))

@@ -8,6 +8,7 @@ SCRATCH = {
     "r0i": ("sbuf", [128, V], "int32"),
     "thi": ("sbuf", [128, 1], "int32"),
     "thb": ("sbuf", [128, 1], "float32"),
+    "thc": ("sbuf", [128, 1], "float32"),
     "nbi": ("sbuf", [128, 256], "int32"),
     "nbu": ("sbuf", [128, 256], "uint16"),
     "sni": ("sbuf", [128, 112], "int32"),
@@ -41,6 +42,18 @@ SEMAPHORES = (["vq", "sq", "pq", "gq", "lsa", "lsb", "lth", "lsn", "lnb", "outp"
 
 STAGES = ((0, 1), (1, 2), (3, 2), (5, 2))
 
+ORD = {
+    "start": {"v": "c0 c1 lst X0 c2 X1 c3 X2 X3 H0 C0 M0 H1 nb C1 M1 C2 M2 C3 M3".split(),
+              "s": "A0 A1 W0 A2 W1 A3 G0 W2 W3 G1 G2 G3 H2 H3".split()},
+    "step": {"v": "ub ua r0 u1 u2 r1 r2 X0 u3 X1 r3 X2 X3 W3 H0 C0 H1 M0 C1 M1 C2 M2 C3 M3".split(),
+             "s": "tb ta t1 t2 A0 t3 A1 W0 A2 W1 A3 G0 G1 W2 G2 G3 H2 H3".split()},
+    "wait": {"v": "d1 d0 b0".split(), "s": "e1 e0 b1".split()},
+    "wait3": {"v": "d1 d0 v1 v0 f1 f0".split(), "s": "e0 e1 b1 b0".split()},
+    "end": {"v": "ua ub u1 r0 r1 u2 r2 u3 r3".split(),
+            "s": "ta tb t1 t2 p0 p1 t3 q0 q1 p2 q2 p3 q3".split()},
+}
+OUT = "p0 p1 q0 q1 p2 q2 p3 q3".split()
+
 
 def order(q, T, topo):
     far = [d for d in range(1, N) if topo.die(T.cores[(q + d) % N]) != topo.die(T.cores[q])]
@@ -70,9 +83,13 @@ def rank_program(g, core, T, topo):
         return
     v, s, pe, sy = g.vector, g.scalar, g.tensor, g.sync
     eng = {"g": g, "v": v, "s": s, "p": pe, "y": sy}
-    cnt, seen = {}, {}
+    cnt, seen, tok = {}, {}, {}
     op, fn = AluOpType, ActivationFunctionType
     LAM = 2.0 ** -21
+    SC = 2.0 ** 22
+    ONE = 1.0 - 2.0 ** -23
+    Q4 = 0.25 * ONE
+    NST = len(STAGES)
 
     def need(k, *toks):
         for name, val in toks:
@@ -88,98 +105,19 @@ def rank_program(g, core, T, topo):
     o, lane = order(q, T, topo), lanes(q, T, topo)
     arrive = sum(len(lanes((q - d) % N, T, topo)[d]) for d in range(1, N))
     C = [slice(512 * c, 512 * c + 512) for c in range(4)]
+    HF = [slice(1024 * h, 1024 * h + 1024) for h in range(2)]
     W = [T["W%d" % t] for t in range(RO)]
     U, E, OB = [T.U0, T.U1], [T.E0, T.E1], [T.ob0, T.ob1]
-    SC = 2.0 ** 22
-    Q4 = 0.25 * (1.0 - 2.0 ** -23)
-
-    lth = fin(s.dma_start(T.thi[:], T.th[:]), "lth", 16)
-    lr = []
-    for c in range(4):
-        lr.append(fin(sy.dma_start(T.r0i[:, C[c]], T.r0[:, C[c]]), "lr%d" % c, 16))
-    lsn = fin(s.dma_start(T.sni[:], T.snd[:]), "lsn", 16)
-    lnb = fin(s.dma_start(T.nbi[:], T.nb[:]), "lnb", 16)
-    k1 = fin(v.memset(T.one[:], 1.0), "vq")
-    kb = fin(v.memset(T.base[:], 5.0), "vq")
-    need("g", k1)
-    k2 = fin(g.affine_select(T.blk1[:], T.one[:], [[-16, 8], [0, 16]], op.is_ge, 0.0, 0, 1), "gq")
-    need("g", k2)
-    kblk = fin(g.affine_select(T.blk[:], T.blk1[:], [[16, 8], [0, 16]], op.is_ge, 0.0, 15, -1), "gq")
-    need("v", kb)
-    fin(v.memset(T.base[:, 0:1], 69.0), "vq")
-    kbase = fin(v.memset(T.base[:, 256:257], 69.0), "vq")
-    need("v", lth)
-    kth = fin(v.tensor_scalar(T.thb[:], T.thi[:], -2.0, 4.0, op.mult, op.add), "vq")
-    need("v", lsn)
-    ksn = None
-    for k in range(N - 1):
-        d = o[k] - 1
-        ksn = fin(v.tensor_copy(T.snu[:, 16 * k:16 * k + 16], T.sni[:, 16 * d:16 * d + 16]), "vq")
-
-    last = {}
-
-    rt, at, xt, wt = [None] * 4, [None] * 4, [None] * 4, [None] * 4
-
-    def fA(c, R):
-        need("s", kth, rt[c])
-        at[c] = fin(s.activation(T.AB[:, C[c]], R[:, C[c]], fn.Relu, bias=T.thb[:], scale=SC), "sq")
-
-    def fX(c, R):
-        need("v", at[c], rt[c], *last.get(("X", c), ()))
-        xt[c] = fin(v.tensor_tensor(T.X[:, C[c]], R[:, C[c]], T.AB[:, C[c]], op.min), "vq")
-
-    def fW(c, t, vec=False):
-        if vec:
-            need("v", xt[c])
-            wt[c] = fin(v.tensor_scalar(W[t][:, C[c]], T.X[:, C[c]], Q4, 4.0, op.mult, op.add), "vq")
-        else:
-            need("s", xt[c])
-            wt[c] = fin(s.activation(W[t][:, C[c]], T.X[:, C[c]], fn.Identity, bias=4.0, scale=Q4), "sq")
-        last[("X", c)] = (wt[c],)
-
-    gt, pt, et, stt, mt = [None] * 4, [None] * 4, [None] * 4, [None] * 4, [None] * 4
+    R = [T.RA, T.RB, T.RB, T.RB, T.RB]
+    PIECE = {"a": (0, 256), "b": (256, 256), "1": (512, 512), "2": (1024, 512), "3": (1536, 512)}
+    left = {}
 
     def cols(i):
         a, n = STAGES[i]
         return slice(G * a, G * (a + n)), slice(16 * a, 16 * (a + n)), slice(512 * i, 512 * i + G * n), G * n
 
-    def fGS(i, R):
-        cs, cl, ch, n = cols(i)
-        need("s", ksn, kth, *rt)
-        need("s", *last.get(("gs", i), ()))
-        gt[i] = fin(s.activation(T.gs[:, cs], R[:, 0:V].indirect(T.snu[:, cl]), fn.Relu, bias=T.thb[:], scale=SC), "sq")
-        need("p", kblk, gt[i], *last.get(("hot", i), ()))
-        pt[i] = fin(pe.matmul(T.hot[:, ch], T.blk[:], T.gs[:, cs], True, True), "pq")
-        last[("gs", i)] = (pt[i],)
-
-    def fEV(i, vec):
-        cs, cl, ch, n = cols(i)
-        k = "v" if vec else "s"
-        need(k, pt[i], *last.get(("hb", i), ()))
-        if vec:
-            et[i] = fin(v.tensor_scalar(T.hb[:, cs], T.hot[:, ch], 0.0, None, op.is_gt), "vq")
-        else:
-            et[i] = fin(s.activation(T.hb[:, cs], T.hot[:, ch], fn.Sign), "sq")
-        last[("hot", i)] = (et[i],)
-
-    def fSCAN(i):
-        cs, cl, ch, n = cols(i)
-        need("v", et[i], kbase)
-        stt[i] = fin(v.tensor_tensor_scan(T.st[:, cs], T.base[:, 0:n], T.hb[:, cs], 69.0, op.max, op.subtract), "vq")
-        last[("hb", i)] = (stt[i],)
-
-    def fGM(i, t):
-        cs, cl, ch, n = cols(i)
-        need("v", stt[i], *wt)
-        if t >= 2:
-            need("v", ("ls" + "ab"[t % 2], left[t - 2]))
-        mt[i] = fin(v.tensor_tensor(OB[t % 2][:, cs], W[t][:, 0:V].indirect(T.snu[:, cl]), T.st[:, cs], op.min), "vq")
-
-    left = {}
-
     def send(i, t):
         a, n = STAGES[i]
-        need("g", mt[i])
         ls = "ls" + "ab"[t % 2]
         tr = []
         for k in range(n):
@@ -199,154 +137,225 @@ def rank_program(g, core, T, topo):
             g.remote_dma_fused(tr, local_sem=T.sem[ls])
         left[t] = cnt[ls]
 
-    def acc(k, buf, *toks):
-        need("g", *toks)
-        return fin(g.dma_start(T.RA[:], buf[:], accum_op=op.add), "acc%d" % k, 16)
-
-    def slots(t, R, steps):
-        for st in steps:
-            if st[0] == "x":
-                fX(st[1], R)
-            elif st[0] == "w":
-                fW(st[1], t, len(st) > 2)
-            elif st[0] == "a":
-                fA(st[1], R)
-            elif st[0] == "g":
-                fGS(st[1], R)
-            elif st[0] == "e":
-                fEV(st[1], len(st) > 2)
-            elif st[0] == "s":
-                fSCAN(st[1])
-            elif st[0] == "m":
-                fGM(st[1], t)
-                send(st[1], t)
-
-    TAIL = (("w", 3, 1), ("e", 0, 1), ("s", 0), ("m", 0), ("g", 1), ("g", 2), ("e", 1, 1), ("s", 1), ("m", 1),
-            ("e", 2), ("g", 3), ("s", 2), ("m", 2), ("e", 3), ("s", 3), ("m", 3))
-
+    tok["th"] = fin(s.dma_start(T.thi[:], T.th[:]), "lth", 16)
     for c in range(4):
-        need("v", lr[c])
-        rt[c] = fin(v.tensor_scalar(T.RA[:, C[c]], T.r0i[:, C[c]], -1.0, LAM, op.add, op.mult), "vq")
-        fA(c, T.RA)
-        fX(c, T.RA)
-        if c < 3:
-            fW(c, 0)
-        else:
-            fGS(0, T.RA)
-    slots(0, T.RA, TAIL)
-    need("v", lnb)
-    knb = fin(v.tensor_copy(T.nbu[:], T.nbi[:]), "vq")
+        tok["l%d" % c] = fin(sy.dma_start(T.r0i[:, C[c]], T.r0[:, C[c]]), "lr%d" % c, 16)
+    tok["sn"] = fin(s.dma_start(T.sni[:], T.snd[:]), "lsn", 16)
+    tok["nbl"] = fin(s.dma_start(T.nbi[:], T.nb[:]), "lnb", 16)
+    k1 = fin(v.memset(T.one[:], 1.0), "vq")
+    kb = fin(v.memset(T.base[:], 5.0), "vq")
+    need("g", k1)
+    k2 = fin(g.affine_select(T.blk1[:], T.one[:], [[-16, 8], [0, 16]], op.is_ge, 0.0, 0, 1), "gq")
+    need("g", k2)
+    tok["blk"] = fin(g.affine_select(T.blk[:], T.blk1[:], [[16, 8], [0, 16]], op.is_ge, 0.0, 15, -1), "gq")
+    need("v", kb)
+    fin(v.memset(T.base[:, 0:1], 69.0), "vq")
+    tok["base"] = fin(v.memset(T.base[:, 256:257], 69.0), "vq")
+    need("v", tok["th"])
+    tok["thb"] = fin(v.tensor_scalar(T.thb[:], T.thi[:], -2.0, 4.0, op.mult, op.add), "vq")
+    tok["thc"] = fin(v.tensor_scalar(T.thc[:], T.thi[:], -1.0, LAM, op.add, op.mult), "vq")
 
-    ae, au = {}, {}
+    def deps(x, t):
+        a, b = x[0], x[1:]
+        al = ["0", "1", "2", "3"]
+        st = [str(i) for i in range(NST)]
+        if a == "c":
+            return ["l" + b]
+        if x == "nb":
+            return ["nbl"]
+        if x == "lst":
+            return ["sn"]
+        if a == "A":
+            return ["thb", "thc", ("r" + b, t - 1)]
+        if a == "X":
+            return [("A" + b, t), ("r" + b, t - 1), ("W" + b, t - 1)]
+        if a == "W":
+            return [("X" + b, t)]
+        if a == "G":
+            return ["thb", "thc", "lst"] + [("r" + c, t - 1) for c in al] + [("P" + b, t - 1)]
+        if a == "P":
+            return ["blk", ("G" + b, t), ("H" + b, t - 1)]
+        if a == "H":
+            return [("P" + b, t), ("C" + b, t - 1)]
+        if a == "C":
+            return ["base", ("H" + b, t), ("M" + b, t - 1)]
+        if a == "M":
+            return [("C" + b, t)] + [("W" + c, t) for c in al] + [("left", t - 2)]
+        if a == "S":
+            return [("M" + b, t)]
+        if a == "d":
+            return [("X" + str(2 * int(b) + h), t) for h in range(2)]
+        if a == "b":
+            return [("d" + b, t)]
+        if a == "e":
+            w2 = [("W" + c, t) for c in (al[:2] if b == "0" else al[2:])]
+            if t == RO - 1:
+                return w2 + [("H" + i, t) for i in st]
+            return w2 + [("Y", t - 2)]
+        if a == "Y":
+            return [("e0", t), ("e1", t), ("d0", t), ("d1", t), ("Z", t - 1)]
+        if a == "Z":
+            return [("Y", t)] + [("u" + c, t) for c in "ab123"]
+        if a == "t":
+            return ["nb", ("arr", t)] + [("W" + c, t) for c in al] + [("u" + b, t - 1)]
+        if a == "u":
+            return ["nb", ("arr", t)] + [("W" + c, t) for c in al] + [("t" + b, t), ("Z", t - 2)]
+        if a == "r":
+            return [("b" + str(int(b) // 2), t)] + [("u" + c, t) for c in ("ab" if b == "0" else b)]
+        if a == "v":
+            return [("e" + b, t), ("Z", t - 1)] + [("W" + c, t) for c in al]
+        if a == "f":
+            return [("v" + b, t), ("b" + b, t), ("Y", t - 1)]
+        if a == "p":
+            return [("f" + str(int(b) // 2), t), ("Y", 1)]
+        if a == "q":
+            return [("r" + b, t)] + [("u" + c, t) for c in ("ab" if b == "0" else b)]
+
+    def call(x, t, k):
+        a, b = x[0], x[1:]
+        c = int(b) if b.isdigit() else None
+        vec = k == "v"
+        if a == "c":
+            return v.tensor_scalar(T.RA[:, C[c]], T.r0i[:, C[c]], -1.0, LAM, op.add, op.mult)
+        if x == "nb":
+            return v.tensor_copy(T.nbu[:], T.nbi[:])
+        if x == "lst":
+            for i in range(N - 1):
+                d = o[i] - 1
+                ins = v.tensor_copy(T.snu[:, 16 * i:16 * i + 16], T.sni[:, 16 * d:16 * d + 16])
+                if i < N - 2:
+                    fin(ins, "vq")
+            return ins
+        if a == "A":
+            if vec:
+                return v.tensor_scalar(T.AB[:, C[c]], R[t][:, C[c]], T.thc[:], 4.0, op.is_ge, op.mult)
+            return s.activation(T.AB[:, C[c]], R[t][:, C[c]], fn.Relu, bias=T.thb[:], scale=SC)
+        if a == "X":
+            return v.tensor_tensor(T.X[:, C[c]], R[t][:, C[c]], T.AB[:, C[c]], op.min)
+        if a == "W":
+            if vec:
+                return v.tensor_scalar(W[t][:, C[c]], T.X[:, C[c]], Q4, 4.0, op.mult, op.add)
+            return s.activation(W[t][:, C[c]], T.X[:, C[c]], fn.Identity, bias=4.0, scale=Q4)
+        if a in "GPHCM":
+            cs, cl, ch, n = cols(c)
+        if a == "G":
+            if vec:
+                return v.tensor_scalar(T.gs[:, cs], R[t][:, 0:V].indirect(T.snu[:, cl]), T.thc[:], None, op.is_ge)
+            return s.activation(T.gs[:, cs], R[t][:, 0:V].indirect(T.snu[:, cl]), fn.Relu, bias=T.thb[:], scale=SC)
+        if a == "P":
+            return pe.matmul(T.hot[:, ch], T.blk[:], T.gs[:, cs], True, True)
+        if a == "H":
+            if vec:
+                return v.tensor_scalar(T.hb[:, cs], T.hot[:, ch], 0.0, None, op.is_gt)
+            return s.activation(T.hb[:, cs], T.hot[:, ch], fn.Sign)
+        if a == "C":
+            return v.tensor_tensor_scan(T.st[:, cs], T.base[:, 0:n], T.hb[:, cs], 69.0, op.max, op.subtract)
+        if a == "M":
+            return v.tensor_tensor(OB[t % 2][:, cs], W[t][:, 0:V].indirect(T.snu[:, cl]), T.st[:, cs], op.min)
+        if a == "d":
+            return v.tensor_tensor(T.AB[:, HF[c]], R[t][:, HF[c]], T.AB[:, HF[c]], op.subtract)
+        if a == "b":
+            if vec:
+                return v.tensor_scalar(T.AB[:, HF[c]], T.AB[:, HF[c]], LAM, 0.0, op.add, op.max)
+            return s.activation(T.AB[:, HF[c]], T.AB[:, HF[c]], fn.Relu, bias=LAM, scale=1.0)
+        if a == "e":
+            out = T.hot if t == RO - 1 else E[t % 2]
+            if vec:
+                return v.tensor_scalar(out[:, HF[c]], W[t][:, HF[c]], -2.0, 8.0, op.mult, op.add)
+            return s.activation(out[:, HF[c]], W[t][:, HF[c]], fn.Identity, bias=8.0, scale=-2.0)
+        if a in "tu":
+            i, n = PIECE[b]
+            cl = slice(i // 16, (i + n) // 16)
+            if a == "t":
+                return s.activation(T.TT[:, i:i + n], W[t][:].indirect(T.nbu[:, 128 + i // 16:128 + (i + n) // 16]), fn.Identity,
+                                    bias=-8.0, scale=ONE)
+            return v.tensor_tensor(U[t % 2][:, i:i + n], W[t][:].indirect(T.nbu[:, cl]), T.TT[:, i:i + n], op.add)
+        if a == "r":
+            return v.tensor_tensor(T.RB[:, C[c]], U[t % 2][:, C[c]], T.AB[:, C[c]], op.add)
+        if a == "v":
+            return v.tensor_tensor(T.X[:, HF[c]], T.RA[:, HF[c]], T.hot[:, HF[c]], op.add)
+        if a == "f":
+            return v.tensor_tensor(T.E0[:, HF[c]], T.X[:, HF[c]], T.AB[:, HF[c]], op.subtract)
+        if a == "p":
+            if vec:
+                return v.tensor_scalar(T.E1[:, C[c]], T.E0[:, C[c]], 1.0 / LAM, 4.0, op.mult, op.add)
+            return s.activation(T.E1[:, C[c]], T.E0[:, C[c]], fn.Identity, bias=4.0, scale=1.0 / LAM)
+        if a == "q":
+            if vec:
+                return v.tensor_scalar(T.TT[:, C[c]], T.RB[:, C[c]], 1.0 / LAM, 1.0, op.mult, op.add)
+            return s.activation(T.TT[:, C[c]], T.RB[:, C[c]], fn.Identity, bias=1.0, scale=1.0 / LAM)
+
+    todo = {k: [] for k in "vspgy"}
+
+    def put(part, t, tn=None):
+        for k in "vs":
+            for x in ORD[part][k]:
+                todo[k].append((x, t if tn is None or x[0] not in "AXWGHCM" else tn))
+
+    def slots(t):
+        for x in [x for x in todo["s"] + todo["v"] if x[0][0] == "G" and x[1] == t]:
+            todo["p"].append(("P" + x[0][1:], t))
+        for x in [x for x in todo["v"] if x[0][0] == "M" and x[1] == t]:
+            todo["g"].append(("S" + x[0][1:], t))
+
+    put("start", 0)
+    slots(0)
+    for t in range(RO - 1):
+        put("wait", t)
+        todo["g"].append(("Y", t))
+        put("step", t, t + 1)
+        todo["g"].append(("Z", t))
+        slots(t + 1)
+    put("wait3", RO - 1)
+    put("end", RO - 1)
+    for x in OUT:
+        todo["y"].append(("o" + x, RO - 1))
     for t in range(RO):
-        R = T.RA if t == 0 else T.RB
-        final = t == RO - 1
-        need("v", *at)
-        need("v", *xt)
-        dt_ = fin(v.tensor_tensor(T.AB[:], R[:], T.AB[:], op.subtract), "vq")
-        need("s", *wt)
-        if not final:
-            if t >= 2:
-                need("s", ae[t - 2])
-            e_t = fin(s.activation(E[t % 2][:], W[t][:, 0:V], fn.Identity, bias=16.0 * 1.0 - 8.0, scale=-2.0), "sq")
-        else:
-            need("s", *et)
-            need("s", *pt)
-            e_t = fin(s.activation(T.hot[:], W[t][:, 0:V], fn.Identity, bias=8.0, scale=-2.0), "sq")
-        need("v", dt_)
-        b_t = fin(v.tensor_scalar(T.AB[:], T.AB[:], -LAM, None, op.max), "vq")
-        if not final:
-            ae[t] = acc(2 * t, E[t % 2], e_t, dt_, *([au[t - 1]] if t else []))
-        else:
-            need("v", e_t, au[t - 1], *last[("X", 0)])
-            need("v", *last[("X", 3)])
-            v1 = fin(v.tensor_tensor(T.X[:], T.RA[:], T.hot[:], op.add), "vq")
-            need("v", v1, b_t)
-            v2 = []
-            for c in range(4):
-                v2.append(fin(v.tensor_tensor(T.E0[:, C[c]], T.X[:, C[c]], T.AB[:, C[c]], op.subtract), "vq"))
-        arr = ("arr%d" % t, arrive)
-        ubuf = U[t % 2]
-        utoks = []
-        tt = {}
+        tok[("arr", t)] = ("arr%d" % t, arrive)
+    head = {k: 0 for k in todo}
 
-        def gt1(a, n):
-            need("s", arr, knb, *wt)
-            tt[a] = fin(s.activation(T.TT[:, a:a + n], W[t][:].indirect(T.nbu[:, 128 + a // 16:128 + (a + n) // 16]), fn.Identity,
-                                     bias=-8.0, scale=1.0), "sq")
+    def known(dp):
+        for x in dp:
+            if isinstance(x, tuple) and x[1] < 0:
+                if x[0][0] != "r":
+                    continue
+                x = "c" + x[0][1:]
+            elif isinstance(x, tuple) and x[0] == "left":
+                yield ("ls" + "ab"[x[1] % 2], left[x[1]]) if ("S%d" % (NST - 1), x[1]) in tok else "missing"
+                continue
+            yield tok.get(x, "missing")
 
-        def gu(a, n):
-            need("v", arr, knb, *wt)
-            need("v", tt[a])
-            if t >= 2:
-                need("v", au[t - 2])
-            utoks.append(fin(v.tensor_tensor(ubuf[:, a:a + n], W[t][:].indirect(T.nbu[:, a // 16:(a + n) // 16]), T.TT[:, a:a + n],
-                                             op.add), "vq"))
-
-        def fR(c):
-            need("v", b_t, *utoks)
-            rt[c] = fin(v.tensor_tensor(T.RB[:, C[c]], ubuf[:, C[c]], T.AB[:, C[c]], op.add), "vq")
-
-        need("s", *last.get("TT", ()))
-        gt1(0, 256)
-        gt1(256, 256)
-        for c in range(1, 4):
-            gt1(512 * c, 512)
-        gu(0, 256)
-        gu(256, 256)
-        gu(512, 512)
-        fR(0)
-        if not final:
-            RN = T.RB
-            fA(0, RN)
-            gu(1024, 512)
-            fR(1)
-            fA(1, RN)
-            fX(0, RN)
-            fW(0, t + 1)
-            gu(1536, 512)
-            fR(2)
-            fA(2, RN)
-            fX(1, RN)
-            fW(1, t + 1)
-            last["TT"] = (utoks[-1],)
-            fR(3)
-            fA(3, RN)
-            fX(2, RN)
-            fX(3, RN)
-            au[t] = acc(2 * t + 1, ubuf, ae[t], *utoks)
-            fGS(0, RN)
-            fW(2, t + 1)
-            slots(t + 1, RN, TAIL)
-        else:
-            def outp(c):
-                need("s", v2[c])
-                tok = fin(s.activation(T.E1[:, C[c]], T.E0[:, C[c]], fn.Identity, bias=0.0, scale=1.0 / LAM), "sq")
-                need("y", tok)
-                fin(sy.dma_start(T.yp[:, C[c]], T.E1[:, C[c]]), "outp", 16)
-
-            def outr(c):
-                need("s", rt[c])
-                tok = fin(s.activation(T.TT[:, C[c]], T.RB[:, C[c]], fn.Identity, bias=1.0, scale=1.0 / LAM), "sq")
-                need("y", tok)
-                fin(sy.dma_start(T.yr[:, C[c]], T.TT[:, C[c]]), "outr", 16)
-
-            need("s", ae[1], ae[2])
-            outp(0)
-            outr(0)
-            gu(1024, 512)
-            fR(1)
-            outp(1)
-            outr(1)
-            gu(1536, 512)
-            fR(2)
-            outp(2)
-            outr(2)
-            fR(3)
-            outp(3)
-            outr(3)
+    more = True
+    while more:
+        more = False
+        for k in "vspgy":
+            while head[k] < len(todo[k]):
+                x, t = todo[k][head[k]]
+                got = list(known(deps(x, t) if k != "y" else [(x[1:], t)]))
+                if "missing" in got:
+                    break
+                need(k, *got)
+                nm = (x, t)
+                if x[0] == "S":
+                    send(int(x[1:]), t)
+                    tok[nm] = None
+                elif x[0] in "YZ":
+                    buf = E[t % 2] if x == "Y" else U[t % 2]
+                    tok[nm] = fin(g.dma_start(T.RA[:], buf[:], accum_op=op.add), "acc%d" % (2 * t + (x == "Z")), 16)
+                elif x[0] == "o":
+                    c = C[int(x[2:])]
+                    if x[1] == "p":
+                        fin(sy.dma_start(T.yp[:, c], T.E1[:, c]), "outp", 16)
+                    else:
+                        fin(sy.dma_start(T.yr[:, c], T.TT[:, c]), "outr", 16)
+                    tok[nm] = None
+                else:
+                    tok[nm] = fin(call(x, t, k), {"v": "vq", "s": "sq", "p": "pq"}[k])
+                    if x[0] == "c" or x in ("nb", "lst"):
+                        tok[x] = tok[nm]
+                head[k] += 1
+                more = True
+    assert all(head[k] == len(todo[k]) for k in todo), [(k, todo[k][head[k]]) for k in todo if head[k] < len(todo[k])]
     need("y", ("outp", cnt["outp"]), ("outr", cnt["outr"]))
-    for name in ("vq", "sq", "pq", "gq"):
-        need("g", (name, cnt[name]))
-    for name in ("lsa", "lsb"):
+    for name in ("vq", "sq", "pq", "gq", "lsa", "lsb"):
         need("g", (name, cnt[name]))

@@ -2,8 +2,11 @@ import numpy as np
 from concourse.bass import DstId, RemoteDMATransfer
 from concourse.mybir import AluOpType, ActivationFunctionType
 
-V, G, N, RO = 2048, 256, 8, 4
+V, G, N, RO, CAP = 2048, 256, 8, 4, 64
 NS = (N - 1) * G
+NC = NS // 16
+PAD = 8
+BIG = 4096.0
 SCRATCH = {
     "r0i": ("sbuf", [128, V], "int32"),
     "thi": ("sbuf", [128, 1], "int32"),
@@ -11,12 +14,21 @@ SCRATCH = {
     "thc": ("sbuf", [128, 1], "float32"),
     "nbi": ("sbuf", [128, 256], "int32"),
     "nbu": ("sbuf", [128, 256], "uint16"),
-    "sni": ("sbuf", [128, 112], "int32"),
-    "snu": ("sbuf", [128, 112], "uint16"),
-    "one": ("sbuf", [128, 128], "bfloat16"),
-    "blk1": ("sbuf", [128, 128], "bfloat16"),
-    "blk": ("sbuf", [128, 128], "bfloat16"),
-    "base": ("sbuf", [128, 512], "bfloat16"),
+    "sni": ("sbuf", [128, NC], "int32"),
+    "snf": ("sbuf", [128, NC], "float32"),
+    "snu": ("sbuf", [128, NC], "uint16"),
+    "qf": ("sbuf", [128, NC], "float32"),
+    "lstu": ("sbuf", [128, NC], "uint16"),
+    "one": ("sbuf", [128, 144], "bfloat16"),
+    "bk1": ("sbuf", [128, 144], "bfloat16"),
+    "bk2": ("sbuf", [128, 144], "bfloat16"),
+    "sel": ("sbuf", [128, 144], "bfloat16"),
+    "tri1": ("sbuf", [128, 128], "bfloat16"),
+    "tri": ("sbuf", [128, 128], "bfloat16"),
+    "blkn": ("sbuf", [128, 128], "bfloat16"),
+    "rm": ("sbuf", [128, NC], "bfloat16"),
+    "hb": ("sbuf", [128, NC], "bfloat16"),
+    "cs": ("sbuf", [128, NC], "bfloat16"),
     "RA": ("sbuf", [128, V], "float32"),
     "RB": ("sbuf", [128, V], "float32"),
     "X": ("sbuf", [128, V], "float32"),
@@ -26,14 +38,12 @@ SCRATCH = {
     "E0": ("sbuf", [128, V], "float32"),
     "E1": ("sbuf", [128, V], "float32"),
     "gs": ("sbuf", [128, NS], "bfloat16"),
-    "hb": ("sbuf", [128, NS], "bfloat16"),
-    "st": ("sbuf", [128, NS], "bfloat16"),
     "ob0": ("sbuf", [128, NS], "float32"),
     "ob1": ("sbuf", [128, NS], "float32"),
-    "W0": ("sbuf", [128, V + NS], "float32"),
-    "W1": ("sbuf", [128, V + NS], "float32"),
-    "W2": ("sbuf", [128, V + NS], "float32"),
-    "W3": ("sbuf", [128, V + NS], "float32"),
+    "W0": ("sbuf", [128, PAD + V + NS], "float32"),
+    "W1": ("sbuf", [128, PAD + V + NS], "float32"),
+    "W2": ("sbuf", [128, PAD + V + NS], "float32"),
+    "W3": ("sbuf", [128, PAD + V + NS], "float32"),
     "AB": ("psum", [128, V], "float32"),
     "hot": ("psum", [128, V], "float32"),
 }
@@ -41,16 +51,17 @@ SEMAPHORES = (["vq", "sq", "pq", "gq", "lsa", "lsb", "lth", "lsn", "lnb", "outp"
               + ["arr%d" % t for t in range(RO)] + ["acc%d" % k for k in range(2 * RO)])
 
 STAGES = ((0, 1), (1, 2), (3, 2), (5, 2))
+PARTS = ((0, 3), (3, 4))
 
 ORD = {
-    "start": {"v": "c0 c1 lst X0 c2 X1 c3 X2 X3 H0 C0 M0 H1 nb C1 M1 C2 M2 C3 M3".split(),
-              "s": "A0 A1 W0 A2 W1 A3 G0 W2 W3 G1 G2 G3 H2 H3".split()},
-    "step": {"v": "ub ua r0 u1 u2 r1 r2 X0 u3 X1 r3 X2 X3 W3 H0 C0 H1 M0 C1 M1 C2 M2 C3 M3".split(),
-             "s": "tb ta t1 t2 A0 t3 A1 W0 A2 W1 A3 G0 G1 W2 G2 G3 H2 H3".split()},
+    "start": {"v": "c0 c1 lst c2 c3 G0 X0 X1 X2 X3 H0 C0 Q0 L0 M1 M3 nb".split(),
+              "s": "A0 A1 A2 A3 G1 W0 W1 W2 W3 M0 M2".split()},
+    "step": {"v": "ub ua r0 u1 u2 r1 u3 r2 r3 G0 X0 X1 X2 X3 H0 C0 Q0 L0 M1 M3".split(),
+             "s": "tb ta t1 t2 t3 A0 A1 A2 A3 G1 W0 W1 W2 W3 M0 M2".split()},
     "wait": {"v": "d1 d0 b0".split(), "s": "e1 e0 b1".split()},
     "wait3": {"v": "d1 d0 v1 v0 f1 f0".split(), "s": "e0 e1 b1 b0".split()},
-    "end": {"v": "ua ub u1 r0 r1 u2 r2 u3 r3".split(),
-            "s": "ta tb t1 t2 p0 p1 t3 q0 q1 p2 q2 p3 q3".split()},
+    "end": {"v": "ua ub u1 r0 u2 r1 r2 u3 r3 p3".split(),
+            "s": "ta tb t1 t2 p0 p1 t3 q0 q1 p2 q2 q3".split()},
 }
 OUT = "p0 p1 q0 q1 p2 q2 p3 q3".split()
 
@@ -105,16 +116,19 @@ def rank_program(g, core, T, topo):
     o, lane = order(q, T, topo), lanes(q, T, topo)
     arrive = sum(len(lanes((q - d) % N, T, topo)[d]) for d in range(1, N))
     C = [slice(512 * c, 512 * c + 512) for c in range(4)]
+    CW = [slice(PAD + 512 * c, PAD + 512 * c + 512) for c in range(4)]
     HF = [slice(1024 * h, 1024 * h + 1024) for h in range(2)]
+    HW = [slice(PAD + 1024 * h, PAD + 1024 * h + 1024) for h in range(2)]
+    ALL = slice(PAD, PAD + V + NS)
     W = [T["W%d" % t] for t in range(RO)]
     U, E, OB = [T.U0, T.U1], [T.E0, T.E1], [T.ob0, T.ob1]
     R = [T.RA, T.RB, T.RB, T.RB, T.RB]
     PIECE = {"a": (0, 256), "b": (256, 256), "1": (512, 512), "2": (1024, 512), "3": (1536, 512)}
+    HC, YC = slice(0, NC), slice(512, 512 + NC)
     left = {}
 
-    def cols(i):
-        a, n = STAGES[i]
-        return slice(G * a, G * (a + n)), slice(16 * a, 16 * (a + n)), slice(512 * i, 512 * i + G * n), G * n
+    def cols(a, n):
+        return slice(G * a, G * (a + n)), slice(16 * a, 16 * (a + n))
 
     def send(i, t):
         a, n = STAGES[i]
@@ -126,7 +140,7 @@ def rank_program(g, core, T, topo):
             ad = topo.addr(dst)
             m = sum(1 << e for e in lane[d])
             src = OB[t % 2][:, G * (a + k):G * (a + k + 1)]
-            out = W[t][:, V + (d - 1) * G:V + d * G]
+            out = W[t][:, PAD + V + (d - 1) * G:PAD + V + d * G]
             cnt[ls] = cnt.get(ls, 0) + len(lane[d])
             if n == 1:
                 g.remote_dma(out, src, T.sem["arr%d" % t], T.sem[ls], ad[1], ad[0], m)
@@ -143,14 +157,16 @@ def rank_program(g, core, T, topo):
     tok["sn"] = fin(s.dma_start(T.sni[:], T.snd[:]), "lsn", 16)
     tok["nbl"] = fin(s.dma_start(T.nbi[:], T.nb[:]), "lnb", 16)
     k1 = fin(v.memset(T.one[:], 1.0), "vq")
-    kb = fin(v.memset(T.base[:], 5.0), "vq")
     need("g", k1)
-    k2 = fin(g.affine_select(T.blk1[:], T.one[:], [[-16, 8], [0, 16]], op.is_ge, 0.0, 0, 1), "gq")
+    k2 = fin(g.affine_select(T.bk1[:], T.one[:], [[-16, 9], [0, 16]], op.is_ge, 0.0, 0, 1), "gq")
+    tok["rm"] = fin(g.affine_select(T.rm[:], T.one[:, 0:NC], [[0, N - 1], [1, 16]], op.is_gt, 0.0, 0, 0), "gq")
     need("g", k2)
-    tok["blk"] = fin(g.affine_select(T.blk[:], T.blk1[:], [[16, 8], [0, 16]], op.is_ge, 0.0, 15, -1), "gq")
-    need("v", kb)
-    fin(v.memset(T.base[:, 0:1], 69.0), "vq")
-    tok["base"] = fin(v.memset(T.base[:, 256:257], 69.0), "vq")
+    k3 = fin(g.affine_select(T.bk2[:], T.bk1[:], [[16, 9], [0, 16]], op.is_ge, 0.0, 15, -1), "gq")
+    need("g", k3)
+    tok["sel"] = fin(g.affine_select(T.sel[:], T.bk2[:], [[0, 9], [1, 16]], op.is_equal, 0.0, -15, 0), "gq")
+    k4 = fin(g.affine_select(T.tri1[:], T.bk2[:, 0:128], [[-1, 128]], op.is_gt, 0.0, 0, 1), "gq")
+    for t in range(RO):
+        tok["pad"] = fin(v.memset(W[t][:, 0:PAD], 4.0), "vq")
     need("v", tok["th"])
     tok["thb"] = fin(v.tensor_scalar(T.thb[:], T.thi[:], -2.0, 4.0, op.mult, op.add), "vq")
     tok["thc"] = fin(v.tensor_scalar(T.thc[:], T.thi[:], -1.0, LAM, op.add, op.mult), "vq")
@@ -158,11 +174,14 @@ def rank_program(g, core, T, topo):
     def deps(x, t):
         a, b = x[0], x[1:]
         al = ["0", "1", "2", "3"]
+        gp = [str(i) for i in range(len(PARTS))]
         st = [str(i) for i in range(NST)]
         if a == "c":
             return ["l" + b]
         if x == "nb":
             return ["nbl"]
+        if x == "mat":
+            return ["mat0"]
         if x == "lst":
             return ["sn"]
         if a == "A":
@@ -174,13 +193,19 @@ def rank_program(g, core, T, topo):
         if a == "G":
             return ["thb", "thc", "lst"] + [("r" + c, t - 1) for c in al] + [("P" + b, t - 1)]
         if a == "P":
-            return ["blk", ("G" + b, t), ("H" + b, t - 1)]
+            return ["sel", ("G" + b, t), ("H0", t - 1)]
         if a == "H":
-            return [("P" + b, t), ("C" + b, t - 1)]
+            return [("P" + i, t) for i in gp] + [("C0", t - 1), ("K0", t - 1)]
         if a == "C":
-            return ["base", ("H" + b, t), ("M" + b, t - 1)]
+            return ["rm", ("H0", t), ("K0", t - 1)]
+        if a == "K":
+            return ["mat", ("C0", t), ("Q0", t - 1)]
+        if a == "Q":
+            return [("K0", t), ("L0", t - 1)]
+        if a == "L":
+            return [("Q0", t)] + [("M" + i, t - 1) for i in st]
         if a == "M":
-            return [("C" + b, t)] + [("W" + c, t) for c in al] + [("left", t - 2)]
+            return ["pad", ("L0", t)] + [("W" + c, t) for c in al] + [("left", t - 2)]
         if a == "S":
             return [("M" + b, t)]
         if a == "d":
@@ -190,10 +215,10 @@ def rank_program(g, core, T, topo):
         if a == "e":
             w2 = [("W" + c, t) for c in (al[:2] if b == "0" else al[2:])]
             if t == RO - 1:
-                return w2 + [("H" + i, t) for i in st]
+                return w2 + [("Q0", t)]
             return w2 + [("Y", t - 2)]
         if a == "Y":
-            return [("e0", t), ("e1", t), ("d0", t), ("d1", t), ("Z", t - 1)]
+            return [("e0", t), ("e1", t), ("d0", t), ("d1", t), ("Z", t - 1)] + [("G" + i, t) for i in gp]
         if a == "Z":
             return [("Y", t)] + [("u" + c, t) for c in "ab123"]
         if a == "t":
@@ -222,10 +247,10 @@ def rank_program(g, core, T, topo):
         if x == "lst":
             for i in range(N - 1):
                 d = o[i] - 1
-                ins = v.tensor_copy(T.snu[:, 16 * i:16 * i + 16], T.sni[:, 16 * d:16 * d + 16])
-                if i < N - 2:
-                    fin(ins, "vq")
-            return ins
+                kk = fin(v.tensor_scalar(T.snf[:, 16 * i:16 * i + 16], T.sni[:, 16 * d:16 * d + 16], PAD - (CAP + 1) * BIG, None,
+                                         op.add), "vq")
+            need("v", kk)
+            return v.tensor_scalar(T.snu[:], T.snf[:], (CAP + 1) * BIG - PAD, None, op.add)
         if a == "A":
             if vec:
                 return v.tensor_scalar(T.AB[:, C[c]], R[t][:, C[c]], T.thc[:], 4.0, op.is_ge, op.mult)
@@ -234,24 +259,35 @@ def rank_program(g, core, T, topo):
             return v.tensor_tensor(T.X[:, C[c]], R[t][:, C[c]], T.AB[:, C[c]], op.min)
         if a == "W":
             if vec:
-                return v.tensor_scalar(W[t][:, C[c]], T.X[:, C[c]], Q4, 4.0, op.mult, op.add)
-            return s.activation(W[t][:, C[c]], T.X[:, C[c]], fn.Identity, bias=4.0, scale=Q4)
-        if a in "GPHCM":
-            cs, cl, ch, n = cols(c)
+                return v.tensor_scalar(W[t][:, CW[c]], T.X[:, C[c]], Q4, 4.0, op.mult, op.add)
+            return s.activation(W[t][:, CW[c]], T.X[:, C[c]], fn.Identity, bias=4.0, scale=Q4)
         if a == "G":
+            cs, cl = cols(*PARTS[c])
             if vec:
                 return v.tensor_scalar(T.gs[:, cs], R[t][:, 0:V].indirect(T.snu[:, cl]), T.thc[:], None, op.is_ge)
             return s.activation(T.gs[:, cs], R[t][:, 0:V].indirect(T.snu[:, cl]), fn.Relu, bias=T.thb[:], scale=SC)
         if a == "P":
-            return pe.matmul(T.hot[:, ch], T.blk[:], T.gs[:, cs], True, True)
+            cs, cl = cols(*PARTS[c])
+            for i in range(16):
+                ins = pe.matmul(T.hot[:, cl], T.sel[:, 15 - i:143 - i], T.gs[:, cs.start + i:cs.stop:16], i == 0, i == 15)
+            return ins
         if a == "H":
-            if vec:
-                return v.tensor_scalar(T.hb[:, cs], T.hot[:, ch], 0.0, None, op.is_gt)
-            return s.activation(T.hb[:, cs], T.hot[:, ch], fn.Sign)
+            return v.tensor_scalar(T.hb[:], T.hot[:, HC], 0.0, None, op.is_gt)
         if a == "C":
-            return v.tensor_tensor_scan(T.st[:, cs], T.base[:, 0:n], T.hb[:, cs], 69.0, op.max, op.subtract)
+            return v.tensor_tensor_scan(T.cs[:], T.rm[:], T.hb[:], 0.0, op.mult, op.add)
+        if a == "K":
+            pe.matmul(T.hot[:, YC], T.tri[:], T.hb[:], True, False)
+            return pe.matmul(T.hot[:, YC], T.blkn[:], T.cs[:], False, True)
+        if a == "Q":
+            return v.tensor_tensor(T.qf[:], T.snf[:], T.hot[:, YC], op.min)
+        if a == "L":
+            return v.tensor_scalar(T.lstu[:], T.qf[:], (CAP + 1) * BIG, 0.0, op.add, op.max)
         if a == "M":
-            return v.tensor_tensor(OB[t % 2][:, cs], W[t][:, 0:V].indirect(T.snu[:, cl]), T.st[:, cs], op.min)
+            cs, cl = cols(*STAGES[c])
+            src = W[t][:, 0:PAD + V].indirect(T.lstu[:, cl])
+            if vec:
+                return v.tensor_copy(OB[t % 2][:, cs], src)
+            return s.activation(OB[t % 2][:, cs], src, fn.Identity)
         if a == "d":
             return v.tensor_tensor(T.AB[:, HF[c]], R[t][:, HF[c]], T.AB[:, HF[c]], op.subtract)
         if a == "b":
@@ -261,15 +297,15 @@ def rank_program(g, core, T, topo):
         if a == "e":
             out = T.hot if t == RO - 1 else E[t % 2]
             if vec:
-                return v.tensor_scalar(out[:, HF[c]], W[t][:, HF[c]], -2.0, 8.0, op.mult, op.add)
-            return s.activation(out[:, HF[c]], W[t][:, HF[c]], fn.Identity, bias=8.0, scale=-2.0)
+                return v.tensor_scalar(out[:, HF[c]], W[t][:, HW[c]], -2.0, 8.0, op.mult, op.add)
+            return s.activation(out[:, HF[c]], W[t][:, HW[c]], fn.Identity, bias=8.0, scale=-2.0)
         if a in "tu":
             i, n = PIECE[b]
             cl = slice(i // 16, (i + n) // 16)
             if a == "t":
-                return s.activation(T.TT[:, i:i + n], W[t][:].indirect(T.nbu[:, 128 + i // 16:128 + (i + n) // 16]), fn.Identity,
-                                    bias=-8.0, scale=ONE)
-            return v.tensor_tensor(U[t % 2][:, i:i + n], W[t][:].indirect(T.nbu[:, cl]), T.TT[:, i:i + n], op.add)
+                return s.activation(T.TT[:, i:i + n], W[t][:, ALL].indirect(T.nbu[:, 128 + i // 16:128 + (i + n) // 16]),
+                                    fn.Identity, bias=-8.0, scale=ONE)
+            return v.tensor_tensor(U[t % 2][:, i:i + n], W[t][:, ALL].indirect(T.nbu[:, cl]), T.TT[:, i:i + n], op.add)
         if a == "r":
             return v.tensor_tensor(T.RB[:, C[c]], U[t % 2][:, C[c]], T.AB[:, C[c]], op.add)
         if a == "v":
@@ -290,15 +326,18 @@ def rank_program(g, core, T, topo):
     def put(part, t, tn=None):
         for k in "vs":
             for x in ORD[part][k]:
-                todo[k].append((x, t if tn is None or x[0] not in "AXWGHCM" else tn))
+                todo[k].append((x, t if tn is None or x[0] not in "AXWGHCQLM" else tn))
 
     def slots(t):
-        for x in [x for x in todo["s"] + todo["v"] if x[0][0] == "G" and x[1] == t]:
-            todo["p"].append(("P" + x[0][1:], t))
-        for x in [x for x in todo["v"] if x[0][0] == "M" and x[1] == t]:
-            todo["g"].append(("S" + x[0][1:], t))
+        for i in range(len(PARTS)):
+            todo["p"].append(("P%d" % i, t))
+        todo["p"].append(("K0", t))
+        for i in range(NST):
+            todo["g"].append(("S%d" % i, t))
 
     put("start", 0)
+    todo["v"].insert(todo["v"].index(("X3", 0)), ("mat", 0))
+    tok["mat0"] = k4
     slots(0)
     for t in range(RO - 1):
         put("wait", t)
@@ -339,6 +378,9 @@ def rank_program(g, core, T, topo):
                 if x[0] == "S":
                     send(int(x[1:]), t)
                     tok[nm] = None
+                elif x == "mat":
+                    fin(v.tensor_scalar(T.blkn[:], T.bk2[:, 0:128], -BIG, None, op.mult), "vq")
+                    tok["mat"] = fin(v.tensor_scalar(T.tri[:], T.tri1[:], BIG, None, op.mult), "vq")
                 elif x[0] in "YZ":
                     buf = E[t % 2] if x == "Y" else U[t % 2]
                     tok[nm] = fin(g.dma_start(T.RA[:], buf[:], accum_op=op.add), "acc%d" % (2 * t + (x == "Z")), 16)

import numpy as np
from concourse.bass import DstId, RemoteDMATransfer
from concourse.mybir import AluOpType, ActivationFunctionType

V, G, N, RO, CAP = 2048, 256, 8, 4, 64
NS = (N - 1) * G
NC = NS // 16
PAD = 8
BIG = 4096.0
SCRATCH = {
    "r0i": ("sbuf", [128, V], "int32"),
    "thi": ("sbuf", [128, 1], "int32"),
    "thb": ("sbuf", [128, 1], "float32"),
    "thc": ("sbuf", [128, 1], "float32"),
    "nbi": ("sbuf", [128, 256], "int32"),
    "nbu": ("sbuf", [128, 256], "uint16"),
    "sni": ("sbuf", [128, NC], "int32"),
    "snf": ("sbuf", [128, NC], "float32"),
    "snu": ("sbuf", [128, NC], "uint16"),
    "qf": ("sbuf", [128, NC], "float32"),
    "lstu": ("sbuf", [128, NC], "uint16"),
    "one": ("sbuf", [128, 144], "bfloat16"),
    "bk1": ("sbuf", [128, 144], "bfloat16"),
    "bk2": ("sbuf", [128, 144], "bfloat16"),
    "sel": ("sbuf", [128, 144], "bfloat16"),
    "tri1": ("sbuf", [128, 128], "bfloat16"),
    "tri": ("sbuf", [128, 128], "bfloat16"),
    "blkn": ("sbuf", [128, 128], "bfloat16"),
    "rm": ("sbuf", [128, NC], "bfloat16"),
    "hb": ("sbuf", [128, NC], "bfloat16"),
    "cs": ("sbuf", [128, NC], "bfloat16"),
    "RA": ("sbuf", [128, V], "float32"),
    "RB": ("sbuf", [128, V], "float32"),
    "X": ("sbuf", [128, V], "float32"),
    "TT": ("sbuf", [128, V], "float32"),
    "U0": ("sbuf", [128, V], "float32"),
    "U1": ("sbuf", [128, V], "float32"),
    "E0": ("sbuf", [128, V], "float32"),
    "E1": ("sbuf", [128, V], "float32"),
    "gs": ("sbuf", [128, NS], "bfloat16"),
    "ob0": ("sbuf", [128, NS], "float32"),
    "ob1": ("sbuf", [128, NS], "float32"),
    "W0": ("sbuf", [128, PAD + V + NS], "float32"),
    "W1": ("sbuf", [128, PAD + V + NS], "float32"),
    "W2": ("sbuf", [128, PAD + V + NS], "float32"),
    "W3": ("sbuf", [128, PAD + V + NS], "float32"),
    "AB": ("psum", [128, V], "float32"),
    "hot": ("psum", [128, V], "float32"),
}
SEMAPHORES = (["vq", "sq", "pq", "gq", "lsa", "lsb", "lth", "lsn", "lnb", "outp", "outr"] + ["lr%d" % c for c in range(4)]
              + ["arr%d" % t for t in range(RO)] + ["acc%d" % k for k in range(2 * RO)])

STAGES = ((0, 1), (1, 2), (3, 2), (5, 2))
PARTS = ((0, 3), (3, 4))

ORD = {
    "start": {"v": "c0 c1 lst c2 c3 G0 X0 X1 X2 X3 H0 C0 Q0 L0 M1 M3 nb".split(),
              "s": "A0 A1 A2 A3 G1 W0 W1 W2 W3 M0 M2".split()},
    "step": {"v": "ub ua r0 u1 u2 r1 u3 r2 r3 G0 X0 X1 X2 X3 H0 C0 Q0 L0 M1 M3".split(),
             "s": "tb ta t1 t2 t3 A0 A1 A2 A3 G1 W0 W1 W2 W3 M0 M2".split()},
    "wait": {"v": "d1 d0 b0".split(), "s": "e1 e0 b1".split()},
    "wait3": {"v": "d1 d0 v1 v0 f1 f0".split(), "s": "e0 e1 b1 b0".split()},
    "end": {"v": "ua ub u1 r0 u2 r1 r2 u3 r3 p3".split(),
            "s": "ta tb t1 t2 p0 p1 t3 q0 q1 p2 q2 q3".split()},
}
OUT = "p0 p1 q0 q1 p2 q2 p3 q3".split()


def order(q, T, topo):
    far = [d for d in range(1, N) if topo.die(T.cores[(q + d) % N]) != topo.die(T.cores[q])]
    near = [d for d in range(1, N) if d not in far]
    far.sort(key=lambda d: abs(d - N // 2))
    o = []
    for k in range(N):
        if k < len(far):
            o.append(far[k])
        if k < len(near):
            o.append(near[k])
    return o


def lanes(q, T, topo):
    o, res = order(q, T, topo), {}
    for first, n in STAGES:
        for k in range(n):
            e = topo.engines(T.cores[q], T.cores[(q + o[first + k]) % N])
            res[o[first + k]] = e[k::n]
    return res


def rank_program(g, core, T, topo):
    q = T.rank_of(core)
    if q is None:
        return
    v, s, pe, sy = g.vector, g.scalar, g.tensor, g.sync
    eng = {"g": g, "v": v, "s": s, "p": pe, "y": sy}
    cnt, seen, tok = {}, {}, {}
    op, fn = AluOpType, ActivationFunctionType
    LAM = 2.0 ** -21
    SC = 2.0 ** 22
    ONE = 1.0 - 2.0 ** -23
    Q4 = 0.25 * ONE
    NST = len(STAGES)

    def need(k, *toks):
        for name, val in toks:
            if seen.get((k, name), 0) < val:
                eng[k].wait_ge(T.sem[name], val)
                seen[(k, name)] = val

    def fin(ins, name, n=1):
        cnt[name] = cnt.get(name, 0) + n
        ins.then_inc(T.sem[name], n)
        return (name, cnt[name])

    o, lane = order(q, T, topo), lanes(q, T, topo)
    arrive = sum(len(lanes((q - d) % N, T, topo)[d]) for d in range(1, N))
    C = [slice(512 * c, 512 * c + 512) for c in range(4)]
    CW = [slice(PAD + 512 * c, PAD + 512 * c + 512) for c in range(4)]
    HF = [slice(1024 * h, 1024 * h + 1024) for h in range(2)]
    HW = [slice(PAD + 1024 * h, PAD + 1024 * h + 1024) for h in range(2)]
    ALL = slice(PAD, PAD + V + NS)
    W = [T["W%d" % t] for t in range(RO)]
    U, E, OB = [T.U0, T.U1], [T.E0, T.E1], [T.ob0, T.ob1]
    R = [T.RA, T.RB, T.RB, T.RB, T.RB]
    PIECE = {"a": (0, 256), "b": (256, 256), "1": (512, 512), "2": (1024, 512), "3": (1536, 512)}
    HC, YC = slice(0, NC), slice(512, 512 + NC)
    left = {}

    def cols(a, n):
        return slice(G * a, G * (a + n)), slice(16 * a, 16 * (a + n))

    def send(i, t):
        a, n = STAGES[i]
        ls = "ls" + "ab"[t % 2]
        tr = []
        for k in range(n):
            d = o[a + k]
            dst = T.cores[(q + d) % N]
            ad = topo.addr(dst)
            m = sum(1 << e for e in lane[d])
            src = OB[t % 2][:, G * (a + k):G * (a + k + 1)]
            out = W[t][:, PAD + V + (d - 1) * G:PAD + V + d * G]
            cnt[ls] = cnt.get(ls, 0) + len(lane[d])
            if n == 1:
                g.remote_dma(out, src, T.sem["arr%d" % t], T.sem[ls], ad[1], ad[0], m)
            else:
                tr.append(RemoteDMATransfer(dst_ids=[DstId(rid=ad[0], pnc=ad[1])], dma_engine_mask=m,
                                            remote_sem=T.sem["arr%d" % t], src=src, dst=out))
        if tr:
            g.remote_dma_fused(tr, local_sem=T.sem[ls])
        left[t] = cnt[ls]

    tok["th"] = fin(s.dma_start(T.thi[:], T.th[:]), "lth", 16)
    for c in range(4):
        tok["l%d" % c] = fin(sy.dma_start(T.r0i[:, C[c]], T.r0[:, C[c]]), "lr%d" % c, 16)
    tok["sn"] = fin(s.dma_start(T.sni[:], T.snd[:]), "lsn", 16)
    tok["nbl"] = fin(s.dma_start(T.nbi[:], T.nb[:]), "lnb", 16)
    k1 = fin(v.memset(T.one[:], 1.0), "vq")
    need("g", k1)
    k2 = fin(g.affine_select(T.bk1[:], T.one[:], [[-16, 9], [0, 16]], op.is_ge, 0.0, 0, 1), "gq")
    tok["rm"] = fin(g.affine_select(T.rm[:], T.one[:, 0:NC], [[0, N - 1], [1, 16]], op.is_gt, 0.0, 0, 0), "gq")
    need("g", k2)
    k3 = fin(g.affine_select(T.bk2[:], T.bk1[:], [[16, 9], [0, 16]], op.is_ge, 0.0, 15, -1), "gq")
    need("g", k3)
    tok["sel"] = fin(g.affine_select(T.sel[:], T.bk2[:], [[0, 9], [1, 16]], op.is_equal, 0.0, -15, 0), "gq")
    k4 = fin(g.affine_select(T.tri1[:], T.bk2[:, 0:128], [[-1, 128]], op.is_gt, 0.0, 0, 1), "gq")
    for t in range(RO):
        tok["pad"] = fin(v.memset(W[t][:, 0:PAD], 4.0), "vq")
    need("v", tok["th"])
    tok["thb"] = fin(v.tensor_scalar(T.thb[:], T.thi[:], -2.0, 4.0, op.mult, op.add), "vq")
    tok["thc"] = fin(v.tensor_scalar(T.thc[:], T.thi[:], -1.0, LAM, op.add, op.mult), "vq")

    def deps(x, t):
        a, b = x[0], x[1:]
        al = ["0", "1", "2", "3"]
        gp = [str(i) for i in range(len(PARTS))]
        st = [str(i) for i in range(NST)]
        if a == "c":
            return ["l" + b]
        if x == "nb":
            return ["nbl"]
        if x == "mat":
            return ["mat0"]
        if x == "lst":
            return ["sn"]
        if a == "A":
            return ["thb", "thc", ("r" + b, t - 1)]
        if a == "X":
            return [("A" + b, t), ("r" + b, t - 1), ("W" + b, t - 1)]
        if a == "W":
            return [("X" + b, t)]
        if a == "G":
            return ["thb", "thc", "lst"] + [("r" + c, t - 1) for c in al] + [("P" + b, t - 1)]
        if a == "P":
            return ["sel", ("G" + b, t), ("H0", t - 1)]
        if a == "H":
            return [("P" + i, t) for i in gp] + [("C0", t - 1), ("K0", t - 1)]
        if a == "C":
            return ["rm", ("H0", t), ("K0", t - 1)]
        if a == "K":
            return ["mat", ("C0", t), ("Q0", t - 1)]
        if a == "Q":
            return [("K0", t), ("L0", t - 1)]
        if a == "L":
            return [("Q0", t)] + [("M" + i, t - 1) for i in st]
        if a == "M":
            return ["pad", ("L0", t)] + [("W" + c, t) for c in al] + [("left", t - 2)]
        if a == "S":
            return [("M" + b, t)]
        if a == "d":
            return [("X" + str(2 * int(b) + h), t) for h in range(2)]
        if a == "b":
            return [("d" + b, t)]
        if a == "e":
            w2 = [("W" + c, t) for c in (al[:2] if b == "0" else al[2:])]
            if t == RO - 1:
                return w2 + [("Q0", t)]
            return w2 + [("Y", t - 2)]
        if a == "Y":
            return [("e0", t), ("e1", t), ("d0", t), ("d1", t), ("Z", t - 1)] + [("G" + i, t) for i in gp]
        if a == "Z":
            return [("Y", t)] + [("u" + c, t) for c in "ab123"]
        if a == "t":
            return ["nb", ("arr", t)] + [("W" + c, t) for c in al] + [("u" + b, t - 1)]
        if a == "u":
            return ["nb", ("arr", t)] + [("W" + c, t) for c in al] + [("t" + b, t), ("Z", t - 2)]
        if a == "r":
            return [("b" + str(int(b) // 2), t)] + [("u" + c, t) for c in ("ab" if b == "0" else b)]
        if a == "v":
            return [("e" + b, t), ("Z", t - 1)] + [("W" + c, t) for c in al]
        if a == "f":
            return [("v" + b, t), ("b" + b, t), ("Y", t - 1)]
        if a == "p":
            return [("f" + str(int(b) // 2), t), ("Y", 1)]
        if a == "q":
            return [("r" + b, t)] + [("u" + c, t) for c in ("ab" if b == "0" else b)]

    def call(x, t, k):
        a, b = x[0], x[1:]
        c = int(b) if b.isdigit() else None
        vec = k == "v"
        if a == "c":
            return v.tensor_scalar(T.RA[:, C[c]], T.r0i[:, C[c]], -1.0, LAM, op.add, op.mult)
        if x == "nb":
            return v.tensor_copy(T.nbu[:], T.nbi[:])
        if x == "lst":
            for i in range(N - 1):
                d = o[i] - 1
                kk = fin(v.tensor_scalar(T.snf[:, 16 * i:16 * i + 16], T.sni[:, 16 * d:16 * d + 16], PAD - (CAP + 1) * BIG, None,
                                         op.add), "vq")
            need("v", kk)
            return v.tensor_scalar(T.snu[:], T.snf[:], (CAP + 1) * BIG - PAD, None, op.add)
        if a == "A":
            if vec:
                return v.tensor_scalar(T.AB[:, C[c]], R[t][:, C[c]], T.thc[:], 4.0, op.is_ge, op.mult)
            return s.activation(T.AB[:, C[c]], R[t][:, C[c]], fn.Relu, bias=T.thb[:], scale=SC)
        if a == "X":
            return v.tensor_tensor(T.X[:, C[c]], R[t][:, C[c]], T.AB[:, C[c]], op.min)
        if a == "W":
            if vec:
                return v.tensor_scalar(W[t][:, CW[c]], T.X[:, C[c]], Q4, 4.0, op.mult, op.add)
            return s.activation(W[t][:, CW[c]], T.X[:, C[c]], fn.Identity, bias=4.0, scale=Q4)
        if a == "G":
            cs, cl = cols(*PARTS[c])
            if vec:
                return v.tensor_scalar(T.gs[:, cs], R[t][:, 0:V].indirect(T.snu[:, cl]), T.thc[:], None, op.is_ge)
            return s.activation(T.gs[:, cs], R[t][:, 0:V].indirect(T.snu[:, cl]), fn.Relu, bias=T.thb[:], scale=SC)
        if a == "P":
            cs, cl = cols(*PARTS[c])
            for i in range(16):
                ins = pe.matmul(T.hot[:, cl], T.sel[:, 15 - i:143 - i], T.gs[:, cs.start + i:cs.stop:16], i == 0, i == 15)
            return ins
        if a == "H":
            return v.tensor_scalar(T.hb[:], T.hot[:, HC], 0.0, None, op.is_gt)
        if a == "C":
            return v.tensor_tensor_scan(T.cs[:], T.rm[:], T.hb[:], 0.0, op.mult, op.add)
        if a == "K":
            pe.matmul(T.hot[:, YC], T.tri[:], T.hb[:], True, False)
            return pe.matmul(T.hot[:, YC], T.blkn[:], T.cs[:], False, True)
        if a == "Q":
            return v.tensor_tensor(T.qf[:], T.snf[:], T.hot[:, YC], op.min)
        if a == "L":
            return v.tensor_scalar(T.lstu[:], T.qf[:], (CAP + 1) * BIG, 0.0, op.add, op.max)
        if a == "M":
            cs, cl = cols(*STAGES[c])
            src = W[t][:, 0:PAD + V].indirect(T.lstu[:, cl])
            if vec:
                return v.tensor_copy(OB[t % 2][:, cs], src)
            return s.activation(OB[t % 2][:, cs], src, fn.Identity)
        if a == "d":
            return v.tensor_tensor(T.AB[:, HF[c]], R[t][:, HF[c]], T.AB[:, HF[c]], op.subtract)
        if a == "b":
            if vec:
                return v.tensor_scalar(T.AB[:, HF[c]], T.AB[:, HF[c]], LAM, 0.0, op.add, op.max)
            return s.activation(T.AB[:, HF[c]], T.AB[:, HF[c]], fn.Relu, bias=LAM, scale=1.0)
        if a == "e":
            out = T.hot if t == RO - 1 else E[t % 2]
            if vec:
                return v.tensor_scalar(out[:, HF[c]], W[t][:, HW[c]], -2.0, 8.0, op.mult, op.add)
            return s.activation(out[:, HF[c]], W[t][:, HW[c]], fn.Identity, bias=8.0, scale=-2.0)
        if a in "tu":
            i, n = PIECE[b]
            cl = slice(i // 16, (i + n) // 16)
            if a == "t":
                return s.activation(T.TT[:, i:i + n], W[t][:, ALL].indirect(T.nbu[:, 128 + i // 16:128 + (i + n) // 16]),
                                    fn.Identity, bias=-8.0, scale=ONE)
            return v.tensor_tensor(U[t % 2][:, i:i + n], W[t][:, ALL].indirect(T.nbu[:, cl]), T.TT[:, i:i + n], op.add)
        if a == "r":
            return v.tensor_tensor(T.RB[:, C[c]], U[t % 2][:, C[c]], T.AB[:, C[c]], op.add)
        if a == "v":
            return v.tensor_tensor(T.X[:, HF[c]], T.RA[:, HF[c]], T.hot[:, HF[c]], op.add)
        if a == "f":
            return v.tensor_tensor(T.E0[:, HF[c]], T.X[:, HF[c]], T.AB[:, HF[c]], op.subtract)
        if a == "p":
            if vec:
                return v.tensor_scalar(T.E1[:, C[c]], T.E0[:, C[c]], 1.0 / LAM, 4.0, op.mult, op.add)
            return s.activation(T.E1[:, C[c]], T.E0[:, C[c]], fn.Identity, bias=4.0, scale=1.0 / LAM)
        if a == "q":
            if vec:
                return v.tensor_scalar(T.TT[:, C[c]], T.RB[:, C[c]], 1.0 / LAM, 1.0, op.mult, op.add)
            return s.activation(T.TT[:, C[c]], T.RB[:, C[c]], fn.Identity, bias=1.0, scale=1.0 / LAM)

    todo = {k: [] for k in "vspgy"}

    def put(part, t, tn=None):
        for k in "vs":
            for x in ORD[part][k]:
                todo[k].append((x, t if tn is None or x[0] not in "AXWGHCQLM" else tn))

    def slots(t):
        for i in range(len(PARTS)):
            todo["p"].append(("P%d" % i, t))
        todo["p"].append(("K0", t))
        for i in range(NST):
            todo["g"].append(("S%d" % i, t))

    put("start", 0)
    todo["v"].insert(todo["v"].index(("X3", 0)), ("mat", 0))
    tok["mat0"] = k4
    slots(0)
    for t in range(RO - 1):
        put("wait", t)
        todo["g"].append(("Y", t))
        put("step", t, t + 1)
        todo["g"].append(("Z", t))
        slots(t + 1)
    put("wait3", RO - 1)
    put("end", RO - 1)
    for x in OUT:
        todo["y"].append(("o" + x, RO - 1))
    for t in range(RO):
        tok[("arr", t)] = ("arr%d" % t, arrive)
    head = {k: 0 for k in todo}

    def known(dp):
        for x in dp:
            if isinstance(x, tuple) and x[1] < 0:
                if x[0][0] != "r":
                    continue
                x = "c" + x[0][1:]
            elif isinstance(x, tuple) and x[0] == "left":
                yield ("ls" + "ab"[x[1] % 2], left[x[1]]) if ("S%d" % (NST - 1), x[1]) in tok else "missing"
                continue
            yield tok.get(x, "missing")

    more = True
    while more:
        more = False
        for k in "vspgy":
            while head[k] < len(todo[k]):
                x, t = todo[k][head[k]]
                got = list(known(deps(x, t) if k != "y" else [(x[1:], t)]))
                if "missing" in got:
                    break
                need(k, *got)
                nm = (x, t)
                if x[0] == "S":
                    send(int(x[1:]), t)
                    tok[nm] = None
                elif x == "mat":
                    fin(v.tensor_scalar(T.blkn[:], T.bk2[:, 0:128], -BIG, None, op.mult), "vq")
                    tok["mat"] = fin(v.tensor_scalar(T.tri[:], T.tri1[:], BIG, None, op.mult), "vq")
                elif x[0] in "YZ":
                    buf = E[t % 2] if x == "Y" else U[t % 2]
                    tok[nm] = fin(g.dma_start(T.RA[:], buf[:], accum_op=op.add), "acc%d" % (2 * t + (x == "Z")), 16)
                elif x[0] == "o":
                    c = C[int(x[2:])]
                    if x[1] == "p":
                        fin(sy.dma_start(T.yp[:, c], T.E1[:, c]), "outp", 16)
                    else:
                        fin(sy.dma_start(T.yr[:, c], T.TT[:, c]), "outr", 16)
                    tok[nm] = None
                else:
                    tok[nm] = fin(call(x, t, k), {"v": "vq", "s": "sq", "p": "pq"}[k])
                    if x[0] == "c" or x in ("nb", "lst"):
                        tok[x] = tok[nm]
                head[k] += 1
                more = True
    assert all(head[k] == len(todo[k]) for k in todo), [(k, todo[k][head[k]]) for k in todo if head[k] < len(todo[k])]
    need("y", ("outp", cnt["outp"]), ("outr", cnt["outr"]))
    for name in ("vq", "sq", "pq", "gq", "lsa", "lsb"):
        need("g", (name, cnt[name]))
